import numpy as np
import ml_dtypes


def mxq(x, axis, fmt="e4m3"):
    dtype, down = {"e4m3": (ml_dtypes.float8_e4m3fn, 7), "e5m2": (ml_dtypes.float8_e5m2, 14)}[fmt]
    v = np.moveaxis(np.asarray(x, np.float32).astype(ml_dtypes.bfloat16).astype(np.float64), axis, -1)
    blocks = v.reshape(v.shape[:-1] + (-1, 32))
    amax = np.abs(blocks).max(-1, keepdims=True)
    byte = np.maximum(np.where(amax > 0, np.frexp(amax)[1] - 1 + 127, 0) - down, 1)
    scale = np.exp2(byte - 127.0)
    codes = (blocks / scale).astype(np.float32).astype(dtype).astype(np.float64)
    return np.moveaxis((codes * scale).reshape(v.shape), -1, axis)


WIDE = False


def mx_kscale(k):
    if not WIDE:
        return np.ones(k)
    levels = np.array([10, -10, 5, -5, 0])
    if k % 512:
        return np.exp2(np.random.permutation(np.resize(levels, k // 32))).repeat(32)
    a = np.empty((k // 512, 16))
    for p in range(k // 512):
        a[p, :8] = np.random.permutation(np.resize(levels, 8))
        for g in range(8):
            far = levels[np.abs(levels - a[p, g]) >= 10]
            a[p, g + 8] = far[np.random.randint(len(far))]
    return np.exp2(a.ravel()).repeat(32)


def f64(x):
    return np.asarray(x).astype(np.float64)


def striped(idx):
    return np.tile(idx.reshape(-1, 16).T, (8, 1)).astype(np.uint16)


def unstriped(offs):
    return offs[:16].T.reshape(-1).astype(np.int64)


def striped8(idx):
    return np.concatenate([x.reshape(-1, 16).T for x in idx]).astype(np.uint16)


def runs(offs, k):
    lists = np.stack([offs[16 * r : 16 * r + 16].T.reshape(-1) for r in range(8)]).astype(np.int64)
    return lists[np.arange(k) % 512 // 64]


def pack_weight(w):
    k, n = w.shape
    w = f64(np.asarray(w, np.float32).astype(ml_dtypes.bfloat16)).reshape(k // 32, 32, n)
    amax = np.abs(w).max(1)
    byte = np.clip(np.where(amax > 0, np.frexp(amax)[1] - 1 + 127 - 7, 1), 1, 254)
    scaled = (w * np.exp2(127.0 - byte)[:, None, :]).reshape(k, n).astype(np.float32)
    words = np.ascontiguousarray(scaled.reshape(k // 512, 128, 4, n).transpose(0, 1, 3, 2)).astype(ml_dtypes.float8_e4m3fn).view(np.uint8)
    return words, np.ascontiguousarray(byte.astype(np.uint8).reshape(k // 512, 16, n))


def unpack_weight(words, scales):
    g, p, n, _ = words.shape
    vals = np.ascontiguousarray(words).view(ml_dtypes.float8_e4m3fn).astype(np.float64) * np.repeat(np.exp2(scales.astype(np.float64) - 127.0), 8, axis=1)[..., None]
    return vals.transpose(0, 1, 3, 2).reshape(g * 512, n)


K, T, S, V, H, C = 512, 2048, 512, 256, 512, 512


def setup_inputs():
    n = np.random.standard_normal
    s = mx_kscale(K)[:, None]
    packed_xT = pack_weight(n((K, T)) * s)
    perm = np.stack([np.random.permutation(S) for _ in range(8)])
    return {
        "x_words": packed_xT[0],
        "x_scales": packed_xT[1],
        "w1": (n((K, H)) / np.sqrt(K) / s).astype(np.float32),
        "gs": (np.random.uniform(0.5, 1.5, (K, 1)) / s).astype(np.float32),
        "offs": striped(np.random.permutation(T)[:S]),
        "la": striped8(perm[:, :V]),
        "lb": striped8(perm[:, V:]),
        "cand": striped(np.random.permutation(T)[:C]),
    }


def reference(x_words, x_scales, w1, gs, offs, la, lb, cand):
    x_cand = unpack_weight(x_words, x_scales)[:, unstriped(cand)]
    xq = unpack_weight(x_words, x_scales)[:, unstriped(offs)]
    h = mxq(f64(w1), 0, "e4m3").T @ xq
    b = h[np.arange(H)[:, None], runs(lb, H)]
    a = h[np.arange(H)[:, None], runs(la, H)]
    mn = 0.5 * (a + b)
    db = np.abs(b - mn)
    d1 = np.zeros((H, S))
    d1[np.arange(H)[:, None], runs(la, H)] = mn
    d2 = d1.copy()
    d2[np.arange(H)[:, None], runs(lb, H)] = db
    z = f64(gs) * d2
    return 0.0625 * ((x_cand.T @ mxq(z, 0, "e4m3")))

@@ -1,0 +1,179 @@
+from contextlib import ExitStack
+
+import concourse.mybir as mybir
+
+F32 = mybir.dt.float32
+BF16 = mybir.dt.bfloat16
+I32 = mybir.dt.int32
+U32 = mybir.dt.uint32
+U16 = mybir.dt.uint16
+U8 = mybir.dt.uint8
+FP8X4 = mybir.dt.float8_e4m3fn_x4
+ACT = mybir.ActivationFunctionType
+ALU = mybir.AluOpType
+
+K, T, S, V, H, C = 512, 2048, 512, 256, 512, 512
+P = 128
+PACK = 4
+HALF = 256
+FLOPS = 2 * K * H * S + 2 * K * C * S
+
+PLANE_ORDER = (2, 0, 1, 3)
+W_SPLIT = 80
+
+
+def tile_picked_candhaar_none_p_kernel(
+    tc, x_words, x_scales, w1, gs, offs, la, lb, cand, out
+):
+    nc = tc.nc
+    with ExitStack() as ctx:
+        keep = ctx.enter_context(tc.tile_pool(name="keep", bufs=1))
+        ring = ctx.enter_context(tc.tile_pool(name="ring", bufs=2))
+        psum = ctx.enter_context(tc.psum_pool(name="psum", bufs=8))
+
+        offs_sb = keep.tile([P, S // 16], U16, name="offs_sb")
+        cand_sb = keep.tile([P, C // 16], U16, name="cand_sb")
+        la_sb = keep.tile([P, V // 16], U16, name="la_sb")
+        lb_sb = keep.tile([P, V // 16], U16, name="lb_sb")
+        table_scales = keep.tile([P, T], U8, name="table_scales", align_bytes=64)
+        table_words = keep.tile([P, T], U32, name="table_words", align_bytes=64)
+        w_raw = keep.tile([P, PACK, H], F32, name="w_raw", align_bytes=64)
+        gs_sb = keep.tile([P, PACK], F32, name="gs_sb")
+
+        nc.vector.memset(table_scales[:].bitcast(I32), 0)
+        nc.sync.dma_start(offs_sb[:], offs)
+        nc.sync.dma_start(cand_sb[:], cand)
+        for q in range(4):
+            nc.sync.dma_start(
+                table_scales[32 * q : 32 * q + 4, :].bitcast(I32),
+                x_scales[0, 4 * q : 4 * q + 4, :].bitcast(I32),
+            )
+        nc.sync.dma_start(w_raw[:], w1.rearrange("(p j) c -> p j c", j=PACK))
+        nc.sync.dma_start(
+            table_words[:].bitcast(I32),
+            x_words[0].rearrange("p n t -> p (n t)").bitcast(I32),
+        )
+        nc.sync.dma_start(la_sb[:], la)
+        nc.sync.dma_start(lb_sb[:], lb)
+        nc.sync.dma_start(gs_sb[:], gs.rearrange("(p t) o -> p (t o)", t=PACK))
+
+        tok_scales = keep.tile([P, S], U8, name="tok_scales", align_bytes=64)
+        cand_scales = keep.tile([P, C], U8, name="cand_scales", align_bytes=64)
+        nc.vector.tensor_copy(tok_scales[:], table_scales[:].indirect(offs_sb[:]))
+        nc.vector.tensor_copy(cand_scales[:], table_scales[:].indirect(cand_sb[:]))
+
+        w_bf = keep.tile([P, PACK, P, PACK], BF16, name="w_bf", align_bytes=64)
+        w_src = w_raw[:].rearrange("p j (m t) -> p m j t", t=PACK)
+        w_dst = w_bf[:].rearrange("p t m j -> p m j t")
+        nc.scalar.activation(w_dst[:, W_SPLIT:], w_src[:, W_SPLIT:], ACT.Copy)
+        nc.vector.tensor_copy(w_dst[:, :W_SPLIT], w_src[:, :W_SPLIT])
+        w_words = keep.tile([P, H], U32, name="w_words", align_bytes=64)
+        w_scales = keep.tile([P, H], U8, name="w_scales", align_bytes=64)
+        nc.vector.quantize_mx(
+            out=w_words[:].bitcast(FP8X4),
+            scales=w_scales[:],
+            in_=w_bf[:].rearrange("p t m j -> p (t m j)"),
+        )
+
+        tok_words = []
+        for u in range(2):
+            words = keep.tile([P, HALF], U32, name=f"tok_words{u}", tag=("w_bf", "tok_words1")[u], align_bytes=64)
+            nc.vector.tensor_copy(words[:], table_words[:].indirect(offs_sb[:, 16 * u : 16 * u + 16]))
+            tok_words.append(words)
+        cand_words = keep.tile([P, C], U32, name="cand_words", align_bytes=64)
+        nc.vector.tensor_copy(cand_words[:], table_words[:].indirect(cand_sb[:]))
+
+        h_half = {}
+        for t in PLANE_ORDER:
+            h_half[t] = keep.tile([P, S], F32, name=f"h_half{t}")
+            for u in range(2):
+                cols = slice(HALF * u, HALF * (u + 1))
+                bank = psum.tile([P, HALF], F32, name="bank")
+                nc.tensor.matmul_mx(
+                    out=bank[:],
+                    lhsT=w_words[:, P * t : P * (t + 1)].bitcast(FP8X4),
+                    lhsT_scale=w_scales[:, P * t : P * (t + 1)],
+                    rhs=tok_words[u][:].bitcast(FP8X4),
+                    rhs_scale=tok_scales[:, cols],
+                    start=True,
+                    stop=True,
+                )
+                nc.scalar.activation(h_half[t][:, cols], bank[:], ACT.Copy, scale=0.5)
+
+        z_bf = [keep.tile([P, HALF, PACK], BF16, name=f"z_bf{u}", align_bytes=64) for u in range(2)]
+        a_half, a_full, diff, size, placed = {}, {}, {}, {}, {}
+
+        def fetch_a(t):
+            a_half[t] = ring.tile([P, V], F32, name="a_half")
+            a_full[t] = ring.tile([P, V], F32, name="a_full")
+            nc.vector.tensor_copy(a_half[t][:], h_half[t][:].indirect(la_sb[:]))
+            nc.scalar.activation(a_full[t][:], a_half[t][:], ACT.Copy, scale=2.0)
+
+        def fetch_diff(t):
+            diff[t] = ring.tile([P, V], F32, name="diff")
+            size[t] = ring.tile([P, V], F32, name="size")
+            nc.vector.tensor_tensor(diff[t][:], h_half[t][:].indirect(lb_sb[:]), a_half[t][:], ALU.subtract)
+            nc.scalar.activation(size[t][:], diff[t][:], ACT.Abs)
+
+        def put_mean(t):
+            placed[t] = ring.tile([P, S], F32, name="placed")
+            nc.vector.tensor_tensor(placed[t][:].indirect(la_sb[:]), a_full[t][:], diff[t][:], ALU.add)
+
+        def put_size(t):
+            nc.vector.tensor_copy(placed[t][:].indirect(lb_sb[:]), size[t][:])
+            for u in range(2):
+                src = placed[t][:, HALF * u : HALF * (u + 1)]
+                if t == PLANE_ORDER[-1] and u == 0:
+                    nc.vector.tensor_scalar(z_bf[u][:, :, t], src, gs_sb[:, t : t + 1], None, ALU.mult)
+                else:
+                    nc.scalar.activation(z_bf[u][:, :, t], src, ACT.Copy, scale=gs_sb[:, t : t + 1])
+
+        p0, p1, p2, p3 = PLANE_ORDER
+        fetch_a(p0)
+        fetch_a(p1)
+        fetch_diff(p0)
+        fetch_diff(p1)
+        put_mean(p0)
+        put_mean(p1)
+        put_size(p0)
+        fetch_a(p2)
+        put_size(p1)
+        fetch_a(p3)
+        fetch_diff(p2)
+        fetch_diff(p3)
+        put_mean(p2)
+        put_mean(p3)
+        put_size(p2)
+        put_size(p3)
+
+        z_words, z_scales = [], []
+        for u in range(2):
+            words = keep.tile([P, HALF], U32, name=f"z_words{u}", align_bytes=64)
+            scales = keep.tile([P, HALF], U8, name=f"z_scales{u}", align_bytes=64)
+            nc.vector.quantize_mx(
+                out=words[:].bitcast(FP8X4),
+                scales=scales[:],
+                in_=z_bf[u][:].rearrange("p n t -> p (n t)"),
+            )
+            z_words.append(words)
+            z_scales.append(scales)
+
+        for u in range(2):
+            for r in range(C // P):
+                rows = slice(P * r, P * (r + 1))
+                bank = psum.tile([P, HALF], F32, name="bank")
+                nc.tensor.matmul_mx(
+                    out=bank[:],
+                    lhsT=cand_words[:, rows].bitcast(FP8X4),
+                    lhsT_scale=cand_scales[:, rows],
+                    rhs=z_words[u][:].bitcast(FP8X4),
+                    rhs_scale=z_scales[u][:],
+                    start=True,
+                    stop=True,
+                )
+                scores = keep.tile([P, HALF], F32, name=f"scores{u}_{r}")
+                if u == 0 and r < 2 or r % 2 == 0:
+                    nc.scalar.activation(scores[:], bank[:], ACT.Copy, scale=0.0625)
+                else:
+                    nc.vector.tensor_scalar(scores[:], bank[:], 0.0625, None, ALU.mult)
+                nc.sync.dma_start(out[rows, HALF * u : HALF * (u + 1)], scores[:])

@@ -20,6 +20,7 @@ FLOPS = 2 * K * H * S + 2 * K * C * S
 
 PLANE_ORDER = (2, 0, 1, 3)
 W_SPLIT = 80
+CHUNKS = ((0, 128), (128, 128), (256, 256))
 
 
 def tile_picked_candhaar_none_p_kernel(
@@ -75,32 +76,31 @@ def tile_picked_candhaar_none_p_kernel(
             in_=w_bf[:].rearrange("p t m j -> p (t m j)"),
         )
 
-        tok_words = []
+        picked = keep.tile([P, S + C], U32, name="picked", tag="w_bf", align_bytes=64)
+        tok_words = [picked[:, HALF * u : HALF * (u + 1)] for u in range(2)]
+        cand_words = picked[:, S:]
         for u in range(2):
-            words = keep.tile([P, HALF], U32, name=f"tok_words{u}", tag=("w_bf", "tok_words1")[u], align_bytes=64)
-            nc.vector.tensor_copy(words[:], table_words[:].indirect(offs_sb[:, 16 * u : 16 * u + 16]))
-            tok_words.append(words)
-        cand_words = keep.tile([P, C], U32, name="cand_words", align_bytes=64)
-        nc.vector.tensor_copy(cand_words[:], table_words[:].indirect(cand_sb[:]))
+            nc.vector.tensor_copy(tok_words[u], table_words[:].indirect(offs_sb[:, 16 * u : 16 * u + 16]))
+        nc.vector.tensor_copy(cand_words, table_words[:].indirect(cand_sb[:]))
 
-        h_half = {}
-        for t in PLANE_ORDER:
-            h_half[t] = keep.tile([P, S], F32, name=f"h_half{t}")
+        h_half = {t: keep.tile([P, S], F32, name=f"h_half{t}") for t in PLANE_ORDER}
+        for pair in (PLANE_ORDER[:2], PLANE_ORDER[2:]):
             for u in range(2):
                 cols = slice(HALF * u, HALF * (u + 1))
-                bank = psum.tile([P, HALF], F32, name="bank")
-                nc.tensor.matmul_mx(
-                    out=bank[:],
-                    lhsT=w_words[:, P * t : P * (t + 1)].bitcast(FP8X4),
-                    lhsT_scale=w_scales[:, P * t : P * (t + 1)],
-                    rhs=tok_words[u][:].bitcast(FP8X4),
-                    rhs_scale=tok_scales[:, cols],
-                    start=True,
-                    stop=True,
-                )
-                nc.scalar.activation(h_half[t][:, cols], bank[:], ACT.Copy, scale=0.5)
+                for t in pair:
+                    bank = psum.tile([P, HALF], F32, name="bank")
+                    nc.tensor.matmul_mx(
+                        out=bank[:],
+                        lhsT=w_words[:, P * t : P * (t + 1)].bitcast(FP8X4),
+                        lhsT_scale=w_scales[:, P * t : P * (t + 1)],
+                        rhs=tok_words[u].bitcast(FP8X4),
+                        rhs_scale=tok_scales[:, cols],
+                        start=True,
+                        stop=True,
+                    )
+                    nc.scalar.activation(h_half[t][:, cols], bank[:], ACT.Copy, scale=0.5)
 
-        z_bf = [keep.tile([P, HALF, PACK], BF16, name=f"z_bf{u}", align_bytes=64) for u in range(2)]
+        z_bf = [keep.tile([P, n, PACK], BF16, name=f"z_bf{c0}", align_bytes=64) for c0, n in CHUNKS]
         a_half, a_full, diff, size, placed = {}, {}, {}, {}, {}
 
         def fetch_a(t):
@@ -121,9 +121,9 @@ def tile_picked_candhaar_none_p_kernel(
 
         def put_size(t):
             nc.vector.tensor_copy(placed[t][:].indirect(lb_sb[:]), size[t][:])
-            for u in range(2):
-                src = placed[t][:, HALF * u : HALF * (u + 1)]
-                if t == PLANE_ORDER[-1] and u == 0:
+            for u, (c0, n) in enumerate(CHUNKS):
+                src = placed[t][:, c0 : c0 + n]
+                if t == PLANE_ORDER[-1] and c0 < HALF:
                     nc.vector.tensor_scalar(z_bf[u][:, :, t], src, gs_sb[:, t : t + 1], None, ALU.mult)
                 else:
                     nc.scalar.activation(z_bf[u][:, :, t], src, ACT.Copy, scale=gs_sb[:, t : t + 1])
@@ -147,9 +147,9 @@ def tile_picked_candhaar_none_p_kernel(
         put_size(p3)
 
         z_words, z_scales = [], []
-        for u in range(2):
-            words = keep.tile([P, HALF], U32, name=f"z_words{u}", align_bytes=64)
-            scales = keep.tile([P, HALF], U8, name=f"z_scales{u}", align_bytes=64)
+        for u, (c0, n) in enumerate(CHUNKS):
+            words = keep.tile([P, n], U32, name=f"z_words{u}", align_bytes=64)
+            scales = keep.tile([P, n], U8, name=f"z_scales{u}", align_bytes=64)
             nc.vector.quantize_mx(
                 out=words[:].bitcast(FP8X4),
                 scales=scales[:],
@@ -158,22 +158,27 @@ def tile_picked_candhaar_none_p_kernel(
             z_words.append(words)
             z_scales.append(scales)
 
-        for u in range(2):
-            for r in range(C // P):
-                rows = slice(P * r, P * (r + 1))
-                bank = psum.tile([P, HALF], F32, name="bank")
-                nc.tensor.matmul_mx(
-                    out=bank[:],
-                    lhsT=cand_words[:, rows].bitcast(FP8X4),
-                    lhsT_scale=cand_scales[:, rows],
-                    rhs=z_words[u][:].bitcast(FP8X4),
-                    rhs_scale=z_scales[u][:],
-                    start=True,
-                    stop=True,
-                )
-                scores = keep.tile([P, HALF], F32, name=f"scores{u}_{r}")
-                if u == 0 and r < 2 or r % 2 == 0:
+        out_blocks = out.rearrange("(r p) j -> p r j", p=P)
+        turn = 0
+        for u, (c0, n) in enumerate(CHUNKS):
+            per_bank = HALF // n
+            for r0 in range(0, C // P, per_bank):
+                bank = psum.tile([P, per_bank, n], F32, name="bank")
+                for i in range(per_bank):
+                    rows = slice(P * (r0 + i), P * (r0 + i + 1))
+                    nc.tensor.matmul_mx(
+                        out=bank[:, i, :],
+                        lhsT=cand_words[:, rows].bitcast(FP8X4),
+                        lhsT_scale=cand_scales[:, rows],
+                        rhs=z_words[u][:].bitcast(FP8X4),
+                        rhs_scale=z_scales[u][:],
+                        start=True,
+                        stop=True,
+                    )
+                scores = keep.tile([P, per_bank, n], F32, name=f"scores{u}_{r0}")
+                if turn % 2 == 0:
                     nc.scalar.activation(scores[:], bank[:], ACT.Copy, scale=0.0625)
                 else:
                     nc.vector.tensor_scalar(scores[:], bank[:], 0.0625, None, ALU.mult)
-                nc.sync.dma_start(out[rows, HALF * u : HALF * (u + 1)], scores[:])
+                nc.sync.dma_start(out_blocks[:, r0 : r0 + per_bank, c0 : c0 + n], scores[:])
+                turn = turn + 1

@@ -158,27 +158,24 @@ def tile_picked_candhaar_none_p_kernel(
             z_words.append(words)
             z_scales.append(scales)
 
-        out_blocks = out.rearrange("(r p) j -> p r j", p=P)
-        turn = 0
-        for u, (c0, n) in enumerate(CHUNKS):
-            per_bank = HALF // n
-            for r0 in range(0, C // P, per_bank):
-                bank = psum.tile([P, per_bank, n], F32, name="bank")
-                for i in range(per_bank):
-                    rows = slice(P * (r0 + i), P * (r0 + i + 1))
-                    nc.tensor.matmul_mx(
-                        out=bank[:, i, :],
-                        lhsT=cand_words[:, rows].bitcast(FP8X4),
-                        lhsT_scale=cand_scales[:, rows],
-                        rhs=z_words[u][:].bitcast(FP8X4),
-                        rhs_scale=z_scales[u][:],
-                        start=True,
-                        stop=True,
-                    )
-                scores = keep.tile([P, per_bank, n], F32, name=f"scores{u}_{r0}")
-                if turn % 2 == 0:
+        for u in range(2):
+            for r in range(C // P):
+                rows = slice(P * r, P * (r + 1))
+                bank = psum.tile([P, HALF], F32, name="bank")
+                for i, (c0, n) in enumerate(CHUNKS):
+                    if c0 // HALF == u:
+                        nc.tensor.matmul_mx(
+                            out=bank[:, c0 % HALF : c0 % HALF + n],
+                            lhsT=cand_words[:, rows].bitcast(FP8X4),
+                            lhsT_scale=cand_scales[:, rows],
+                            rhs=z_words[i][:].bitcast(FP8X4),
+                            rhs_scale=z_scales[i][:],
+                            start=True,
+                            stop=True,
+                        )
+                scores = keep.tile([P, HALF], F32, name=f"scores{u}_{r}")
+                if r % 2 == 0:
                     nc.scalar.activation(scores[:], bank[:], ACT.Copy, scale=0.0625)
                 else:
                     nc.vector.tensor_scalar(scores[:], bank[:], 0.0625, None, ALU.mult)
-                nc.sync.dma_start(out_blocks[:, r0 : r0 + per_bank, c0 : c0 + n], scores[:])
-                turn = turn + 1
+                nc.sync.dma_start(out[rows, HALF * u : HALF * (u + 1)], scores[:])

from contextlib import ExitStack

import concourse.mybir as mybir

F32 = mybir.dt.float32
BF16 = mybir.dt.bfloat16
I32 = mybir.dt.int32
U32 = mybir.dt.uint32
U16 = mybir.dt.uint16
U8 = mybir.dt.uint8
FP8X4 = mybir.dt.float8_e4m3fn_x4
ACT = mybir.ActivationFunctionType
ALU = mybir.AluOpType

K, T, S, V, H, C = 512, 2048, 512, 256, 512, 512
P = 128
PACK = 4
HALF = 256
FLOPS = 2 * K * H * S + 2 * K * C * S

PLANE_ORDER = (2, 0, 1, 3)
W_SPLIT = 80
CHUNKS = ((0, 128), (128, 128), (256, 256))


def tile_picked_candhaar_none_p_kernel(
    tc, x_words, x_scales, w1, gs, offs, la, lb, cand, out
):
    nc = tc.nc
    with ExitStack() as ctx:
        keep = ctx.enter_context(tc.tile_pool(name="keep", bufs=1))
        ring = ctx.enter_context(tc.tile_pool(name="ring", bufs=2))
        psum = ctx.enter_context(tc.psum_pool(name="psum", bufs=8))

        offs_sb = keep.tile([P, S // 16], U16, name="offs_sb")
        cand_sb = keep.tile([P, C // 16], U16, name="cand_sb")
        la_sb = keep.tile([P, V // 16], U16, name="la_sb")
        lb_sb = keep.tile([P, V // 16], U16, name="lb_sb")
        table_scales = keep.tile([P, T], U8, name="table_scales", align_bytes=64)
        table_words = keep.tile([P, T], U32, name="table_words", align_bytes=64)
        w_raw = keep.tile([P, PACK, H], F32, name="w_raw", align_bytes=64)
        gs_sb = keep.tile([P, PACK], F32, name="gs_sb")

        nc.vector.memset(table_scales[:].bitcast(I32), 0)
        nc.sync.dma_start(offs_sb[:], offs)
        nc.sync.dma_start(cand_sb[:], cand)
        for q in range(4):
            nc.sync.dma_start(
                table_scales[32 * q : 32 * q + 4, :].bitcast(I32),
                x_scales[0, 4 * q : 4 * q + 4, :].bitcast(I32),
            )
        nc.sync.dma_start(w_raw[:], w1.rearrange("(p j) c -> p j c", j=PACK))
        nc.sync.dma_start(
            table_words[:].bitcast(I32),
            x_words[0].rearrange("p n t -> p (n t)").bitcast(I32),
        )
        nc.sync.dma_start(la_sb[:], la)
        nc.sync.dma_start(lb_sb[:], lb)
        nc.sync.dma_start(gs_sb[:], gs.rearrange("(p t) o -> p (t o)", t=PACK))

        tok_scales = keep.tile([P, S], U8, name="tok_scales", align_bytes=64)
        cand_scales = keep.tile([P, C], U8, name="cand_scales", align_bytes=64)
        nc.vector.tensor_copy(tok_scales[:], table_scales[:].indirect(offs_sb[:]))
        nc.vector.tensor_copy(cand_scales[:], table_scales[:].indirect(cand_sb[:]))

        w_bf = keep.tile([P, PACK, P, PACK], BF16, name="w_bf", align_bytes=64)
        w_src = w_raw[:].rearrange("p j (m t) -> p m j t", t=PACK)
        w_dst = w_bf[:].rearrange("p t m j -> p m j t")
        nc.scalar.activation(w_dst[:, W_SPLIT:], w_src[:, W_SPLIT:], ACT.Copy)
        nc.vector.tensor_copy(w_dst[:, :W_SPLIT], w_src[:, :W_SPLIT])
        w_words = keep.tile([P, H], U32, name="w_words", align_bytes=64)
        w_scales = keep.tile([P, H], U8, name="w_scales", align_bytes=64)
        nc.vector.quantize_mx(
            out=w_words[:].bitcast(FP8X4),
            scales=w_scales[:],
            in_=w_bf[:].rearrange("p t m j -> p (t m j)"),
        )

        picked = keep.tile([P, S + C], U32, name="picked", tag="w_bf", align_bytes=64)
        tok_words = [picked[:, HALF * u : HALF * (u + 1)] for u in range(2)]
        cand_words = picked[:, S:]
        for u in range(2):
            nc.vector.tensor_copy(tok_words[u], table_words[:].indirect(offs_sb[:, 16 * u : 16 * u + 16]))
        nc.vector.tensor_copy(cand_words, table_words[:].indirect(cand_sb[:]))

        h_half = {t: keep.tile([P, S], F32, name=f"h_half{t}") for t in PLANE_ORDER}
        for pair in (PLANE_ORDER[:2], PLANE_ORDER[2:]):
            for u in range(2):
                cols = slice(HALF * u, HALF * (u + 1))
                for t in pair:
                    bank = psum.tile([P, HALF], F32, name="bank")
                    nc.tensor.matmul_mx(
                        out=bank[:],
                        lhsT=w_words[:, P * t : P * (t + 1)].bitcast(FP8X4),
                        lhsT_scale=w_scales[:, P * t : P * (t + 1)],
                        rhs=tok_words[u].bitcast(FP8X4),
                        rhs_scale=tok_scales[:, cols],
                        start=True,
                        stop=True,
                    )
                    nc.scalar.activation(h_half[t][:, cols], bank[:], ACT.Copy, scale=0.5)

        z_bf = [keep.tile([P, n, PACK], BF16, name=f"z_bf{c0}", align_bytes=64) for c0, n in CHUNKS]
        a_half, a_full, diff, size, placed = {}, {}, {}, {}, {}

        def fetch_a(t):
            a_half[t] = ring.tile([P, V], F32, name="a_half")
            a_full[t] = ring.tile([P, V], F32, name="a_full")
            nc.vector.tensor_copy(a_half[t][:], h_half[t][:].indirect(la_sb[:]))
            nc.scalar.activation(a_full[t][:], a_half[t][:], ACT.Copy, scale=2.0)

        def fetch_diff(t):
            diff[t] = ring.tile([P, V], F32, name="diff")
            size[t] = ring.tile([P, V], F32, name="size")
            nc.vector.tensor_tensor(diff[t][:], h_half[t][:].indirect(lb_sb[:]), a_half[t][:], ALU.subtract)
            nc.scalar.activation(size[t][:], diff[t][:], ACT.Abs)

        def put_mean(t):
            placed[t] = ring.tile([P, S], F32, name="placed")
            nc.vector.tensor_tensor(placed[t][:].indirect(la_sb[:]), a_full[t][:], diff[t][:], ALU.add)

        def put_size(t):
            nc.vector.tensor_copy(placed[t][:].indirect(lb_sb[:]), size[t][:])
            for u, (c0, n) in enumerate(CHUNKS):
                src = placed[t][:, c0 : c0 + n]
                if t == PLANE_ORDER[-1] and c0 < HALF:
                    nc.vector.tensor_scalar(z_bf[u][:, :, t], src, gs_sb[:, t : t + 1], None, ALU.mult)
                else:
                    nc.scalar.activation(z_bf[u][:, :, t], src, ACT.Copy, scale=gs_sb[:, t : t + 1])

        p0, p1, p2, p3 = PLANE_ORDER
        fetch_a(p0)
        fetch_a(p1)
        fetch_diff(p0)
        fetch_diff(p1)
        put_mean(p0)
        put_mean(p1)
        put_size(p0)
        fetch_a(p2)
        put_size(p1)
        fetch_a(p3)
        fetch_diff(p2)
        fetch_diff(p3)
        put_mean(p2)
        put_mean(p3)
        put_size(p2)
        put_size(p3)

        z_words, z_scales = [], []
        for u, (c0, n) in enumerate(CHUNKS):
            words = keep.tile([P, n], U32, name=f"z_words{u}", align_bytes=64)
            scales = keep.tile([P, n], U8, name=f"z_scales{u}", align_bytes=64)
            nc.vector.quantize_mx(
                out=words[:].bitcast(FP8X4),
                scales=scales[:],
                in_=z_bf[u][:].rearrange("p n t -> p (n t)"),
            )
            z_words.append(words)
            z_scales.append(scales)

        for u in range(2):
            for r in range(C // P):
                rows = slice(P * r, P * (r + 1))
                bank = psum.tile([P, HALF], F32, name="bank")
                for i, (c0, n) in enumerate(CHUNKS):
                    if c0 // HALF == u:
                        nc.tensor.matmul_mx(
                            out=bank[:, c0 % HALF : c0 % HALF + n],
                            lhsT=cand_words[:, rows].bitcast(FP8X4),
                            lhsT_scale=cand_scales[:, rows],
                            rhs=z_words[i][:].bitcast(FP8X4),
                            rhs_scale=z_scales[i][:],
                            start=True,
                            stop=True,
                        )
                scores = keep.tile([P, HALF], F32, name=f"scores{u}_{r}")
                if r % 2 == 0:
                    nc.scalar.activation(scores[:], bank[:], ACT.Copy, scale=0.0625)
                else:
                    nc.vector.tensor_scalar(scores[:], bank[:], 0.0625, None, ALU.mult)
                nc.sync.dma_start(out[rows, HALF * u : HALF * (u + 1)], scores[:])
